import numpy as np, ml_dtypes
CORES = [2,3,42,43,82,83,122,123]
N = 8
import mx_ref
BF = ml_dtypes.bfloat16
def entries(a):
    return np.ascontiguousarray(a.T).reshape(-1)
def table(e):
    return np.ascontiguousarray(np.reshape(e, (-1, 16)).T).astype(np.int32)
def f(rng, *shape):
    return mx_ref.flush((rng.standard_normal(shape, dtype=np.float32) * np.exp2(rng.integers(-2, 3, shape[:-1] + (1,)))).astype(BF))
def wide(rng, *shape, cols=0):
    v = rng.standard_normal(shape, dtype=np.float32) * np.exp2(rng.integers(-12, 13, shape)).astype(np.float32)
    if cols: v *= np.repeat(np.exp2(rng.integers(-cols, cols + 1, shape[:-2] + (1, shape[-1] // 4))) * (rng.random(shape[:-2] + (1, shape[-1] // 4)) > 0.0625), 4, axis=-1).astype(np.float32)
    return mx_ref.flush(v.astype(BF))
T = 1024
def listed(a):
    k = np.full((2 * N, 128), -1)
    for s in range(2 * N):
        i = np.flatnonzero(a == s); k[s, :len(i)] = i
    return k.reshape(-1)
def lists(rng, one=False, absent=False, sort=False, alike=False):
    t, a, k = [], [], []; nobody = rng.integers(0, N)
    for r in range(N):
        if r == 0 or not alike:
            u = np.concatenate([rng.permutation(8)[:2] for q in range(N)])
            if absent:
                here = rng.permutation([q for q in range(N) if q != nobody])[:T // 256 + r % 3].tolist()
                u.reshape(N, 2)[[q for q in range(N) if q not in here]] = -1
            else: u[rng.permutation(2 * N)[:rng.integers(0, 5)]] = -1
        v = rng.permutation(np.flatnonzero(u >= 0))
        if one: e = np.concatenate([np.full(128, v[0]), np.resize(v[1:], T - 128)])
        else:
            room = np.zeros(2 * N, int); room[v] = rng.integers(0, 129, len(v))
            for s in v:
                if room.sum() < T: room[s] = 128
            e = np.repeat(np.arange(2 * N), room)
        e = rng.permutation(e)[:T]
        if sort: e = np.sort(e)
        t.append(table(u)); a.append(table(e)); k.append(table(listed(e)))
    return {"tab": np.stack(t), "ad": np.stack(a), "tok": np.stack(k)}
def setup_inputs(rng):
    return {"x": f(rng, N, 128, 4 * T), "wa": f(rng, N, 1024, 512), **lists(rng)}
def setup_inputs_absent(rng):
    return {**setup_inputs(rng), **lists(rng, absent=True)}
def setup_inputs_alike(rng):
    return {**setup_inputs(rng), **lists(rng, alike=True)}
def setup_inputs_one(rng):
    return {**setup_inputs(rng), **lists(rng, one=True)}
def setup_inputs_sorted(rng):
    return {**setup_inputs(rng), **lists(rng, sort=True)}
def setup_inputs_spread(rng):
    d = setup_inputs(rng); d["x"] = wide(rng, N, 128, 4 * T, cols=8); return d
def check_inputs(d):
    b = []
    for n in ("x", "wa"):
        v = np.abs(np.asarray(d[n]).astype(np.float32))
        if not ((v == 0) | ((v >= 2.0 ** -30) & (v <= 2.0 ** 30))).all(): b.append(n)
    for r in range(N):
        u, a, k = entries(d["tab"][r]), entries(d["ad"][r]), entries(d["tok"][r]); p = u.reshape(N, 2)
        if u.min() < -1 or u.max() > 7 or ((p[:, 0] == p[:, 1]) & (p[:, 0] >= 0)).any(): b.append("tab")
        if a.min() < 0 or a.max() >= 2 * N or (u[a] < 0).any() or np.bincount(a).max() > 128: b.append("ad")
        elif (k != listed(a)).any(): b.append("tok")
    return b
def reference(x, wa, tab, ad, tok):
    y = np.zeros((N, 128, T), np.float32)
    for r in range(N):
        u, a, X = entries(tab[r]), entries(ad[r]), mx_ref.quantize(x[r])
        for s in range(2 * N):
            i = np.flatnonzero(a == s)
            if len(i) == 0: continue
            A = wa[s // 2][128 * u[s]:128 * u[s] + 128]
            y[r][:, i] = mx_ref.matmul(mx_ref.quantize(A), X)[:, i]
    return {"y": y}

@@ -1,0 +1,354 @@
+from concourse.bass import DstId, RemoteDMATransfer
+from concourse.mybir import dt, AluOpType, ActivationFunctionType
+
+U8 = dt.uint8
+ADD, MUL, MAX, AND = AluOpType.add, AluOpType.mult, AluOpType.max, AluOpType.bitwise_and
+COPY = ActivationFunctionType.Copy
+SSH = 1280
+
+F8 = "float8_e4m3fn_x4"
+I16 = ("sbuf", [128, 16], "int32")
+SCRATCH = {
+    "tabd": ("dram", [128, 1], "int32"), "tabl": ("dram", [8, 128, 1], "int32"), "rtab": ("dram", [128, 1], "int32"),
+    "tv1": ("sbuf", [128, 12], "int32"), "tb1": ("sbuf", [128, 12], "int32"), "mf1": ("sbuf", [128, 12], "float32"),
+    "tv2": ("sbuf", [128, 4], "int32"), "tb2": ("sbuf", [128, 4], "int32"), "mf2": ("sbuf", [128, 4], "float32"),
+    "ibp": ("sbuf", [128, 32], "int32"), "ibc": ("sbuf", [128, 32], "int32"), "ibr": ("sbuf", [128, 32], "int32"),
+    "base": ("sbuf", [128, 32], "float32"), "offu": ("sbuf", [128, 512], "uint16"),
+    "tokb": ("sbuf", [128, 128], "int32"), "xo": ("sbuf", [128, 128], "uint16"),
+    "tk2": I16, "ka": I16, "kb": I16, "km": I16, "ka2": I16, "kmu": I16, "kc": I16, "kd": I16, "ut": I16,
+    "so": ("sbuf", [128, 16], "uint16"), "vals": ("sbuf", [128, 256], "float32"), "inv": ("sbuf", [128, 1392], "float32"),
+    "e2": ("dram", [16, 8, 64], "float32"), "mg": ("sbuf", [128, 512], "float32"), "s1": ("sbuf", [128, 256], "float32"),
+    "s2": ("sbuf", [128, 128], "float32"), "s3": ("sbuf", [128, 64], "float32"), "yo": ("sbuf", [128, 64], "uint16"),
+    "wab": ("sbuf", [128, 4096], "bfloat16"), "xsb": ("sbuf", [128, 4096], "bfloat16"), "hx": ("sbuf", [128, 8192], "bfloat16"),
+    "xq": ("sbuf", [128, 2048], F8), "xp": ("sbuf", [128, 2048], "uint8"),
+    "ga": ("sbuf", [128, 8192], "bfloat16"), "aq": ("sbuf", [128, 1792], F8), "apl": ("sbuf", [128, 1792], "uint8"),
+    "lc": ("sbuf", [128, 2048], F8), "lp": ("sbuf", [128, 2048], "uint8"),
+    "rlc": ("sbuf", [128, 768], F8), "rlp": ("sbuf", [128, 768], "uint8"),
+    "rsb": ("sbuf", [128, 2048], "float32"), "ysb": ("sbuf", [128, 1024], "float32"),
+    "ps": ("psum", [128, 4096], "float32"),
+}
+SEMAPHORES = (["d_tab", "d_own", "d_x", "d_tok", "d_tk2", "d_wa", "d_e1", "d_e2", "d_r1", "d_r2", "d_y",
+               "v", "s", "p", "gq", "lleft", "sent", "m_list", "m_nl", "rl"]
+              + ["arr%d" % q for q in range(8)] + ["rc%d" % t for t in range(3)] + ["rs%d" % t for t in range(3)])
+
+
+def bits(engines):
+    return sum(1 << e for e in engines)
+
+
+def layout(T, topo):
+    chips = []
+    for c in T.cores:
+        if topo.chip(c) not in chips:
+            chips.append(topo.chip(c))
+    ranks = [[r for r, c in enumerate(T.cores) if topo.chip(c) == ch] for ch in chips]
+    steps = sorted(range(1, len(chips)), key=lambda o: topo.same_plane(chips[0], chips[o]))
+    return chips, ranks, steps
+
+
+def relay_of(T, topo, core, place):
+    c = [k for k in topo.cores_of(core) if topo.die(k) != topo.die(core) and T.rank_of(k) is None
+         and all(topo.may_write(k, d) for d in T.cores)]
+    return c[place]
+
+
+def served(ranks, steps, h, i):
+    n = len(ranks)
+    return [(ranks[(h + o) % n][i], ranks[(h + o) % n][1 - i]) for o in steps]
+
+
+def relay_program(g, core, T, topo):
+    chips, ranks, steps = layout(T, topo)
+    if topo.chip(core) not in chips:
+        return
+    h = chips.index(topo.chip(core))
+    for i, r in enumerate(ranks[h]):
+        if relay_of(T, topo, T.cores[r], i) != core:
+            continue
+        me = T.sem
+        nb = T.cores[ranks[h][1 - i]]
+        dests = [T.cores[far] for near, far in served(ranks, steps, h, i)]
+        eng = topo.engines(core, dests[0])
+        on = topo.engines(T.cores[r], core)
+        ins = len([e for e in on if e not in topo.engines(T.cores[r], dests[0])])
+        g.wait_ge(me.rl, len(on))
+        rid, pid, _ = topo.addr(nb)
+        g.remote_dma(T.tabl[6], T.rtab[:], me.m_nl, me.sent, pid, rid, bits(eng))
+        n = len(eng)
+        for t, d in enumerate(dests):
+            rid, pid, _ = topo.addr(d)
+            a, b, c0, c1 = 256 * r, 256 * r + 256, 256 * t, 256 * t + 256
+            g.wait_ge(me["rc%d" % t], ins)
+            g.remote_dma(T.lc[:, a:b].bitcast(U8), T.rlc[:, c0:c1].bitcast(U8), me["arr%d" % r], me.sent, pid, rid, bits(eng))
+            g.wait_ge(me["rs%d" % t], ins)
+            g.remote_dma(T.lp[:, a:b], T.rlp[:, c0:c1], me["arr%d" % r], me.sent, pid, rid, bits(eng))
+            n += 2 * len(eng)
+        g.wait_ge(me.sent, n)
+
+
+def rank_program(g, core, T, topo):
+    rank = T.rank_of(core)
+    if rank is None:
+        return relay_program(g, core, T, topo)
+    chips, ranks, steps = layout(T, topo)
+    C = len(chips)
+    h = chips.index(topo.chip(core))
+    i = ranks[h].index(rank)
+    nbr = ranks[h][1 - i]
+    relay = relay_of(T, topo, core, i)
+    out = served(ranks, steps, h, i)
+    src = [(ranks[(h - o) % C][i], ranks[(h - o) % C][1 - i]) for o in steps]
+    on = topo.engines(core, relay)
+    off = topo.engines(core, T.cores[out[0][0]])
+    inner = [e for e in on if e not in off]
+    S, V, P, Y = g.scalar, g.vector, g.tensor, g.sync
+    m = T.sem
+    cnt = {"v": 0, "s": 0, "p": 0, "gq": 0, "sent": 0}
+
+    def did(ins, name):
+        ins.then_inc(m[name], 1)
+        cnt[name] += 1
+        return cnt[name]
+
+    def v(ins): return did(ins, "v")
+    def s(ins): return did(ins, "s")
+    def gq(ins): return did(ins, "gq")
+
+    def place(q):
+        hq = [k for k in range(C) if q in ranks[k]][0]
+        o = served(ranks, steps, hq, ranks[hq].index(q))
+        return [2 * t + k for t in range(len(o)) for k in range(2) if o[t][k] == rank][0]
+
+    Y.dma_start(T.tabd[0:16, :], T.tab[:]).then_inc(m.d_tab, 16)
+    Y.dma_start(T.tabd[16:128, :], T.tok[0:1, 0:112]).then_inc(m.d_tab, 16)
+    Y.dma_start(T.xsb[:], T.x[:]).then_inc(m.d_x, 16)
+    Y.dma_start(T.tabl[7, 0:16, :], T.tab[:]).then_inc(m.d_own, 16)
+    for k in range(8):
+        S.dma_start(T.tk2[16 * k:16 * k + 16, :], T.tok[:, 16 * k:16 * k + 16]).then_inc(m.d_tk2, 16)
+    for k in range(8):
+        S.dma_start(T.tokb[16 * k:16 * k + 16, :], T.tok[:]).then_inc(m.d_tok, 16)
+    gq(g.iota(T.ut[:], [[16, 16]], 65, 1))
+    gq(g.iota(T.vals[:], [[1, 256]], 0, 16, allow_small_or_imprecise_dtypes=True))
+    gq(g.iota(T.ibp[:], [[0, 32]], 0, 1))
+    g_b = gq(g.iota(T.ibc[:], [[16, 32]], 0, 0))
+    g.wait_ge(m.d_tab, 32)
+    far = [q for pair in out for q in pair]
+    ids, dsts = [], []
+    for q in far:
+        rid, pid, _ = topo.addr(T.cores[q])
+        ids.append(DstId(rid=rid, pnc=pid))
+        dsts.append(T.tabl[place(q)])
+    g.remote_dma_fused([RemoteDMATransfer(dst_ids=ids, dma_engine_mask=bits(off[:1]), remote_sem=m.m_list,
+                                          srcs=[T.tabd[:]], dsts=dsts)], local_sem=m.lleft)
+    rid, pid, _ = topo.addr(relay)
+    rly = DstId(rid=rid, pnc=pid)
+    g.remote_dma(T.rtab[:], T.tabd[:], m.rl, m.sent, pid, rid, bits(on))
+    cnt["sent"] += len(on)
+
+    v(V.memset(T.inv[:], 0.0))
+    V.wait_ge(m.gq, g_b)
+    n = v(V.tensor_scalar(T.ibr[:], T.ibp[:], 15, None, AND))
+    V.wait_ge(m.v, n)
+    v(V.tensor_tensor(T.base[:], T.ibr[:], T.ibc[:], ADD))
+    V.wait_ge(m.d_tk2, 128)
+    v(V.tensor_scalar(T.ka[:], T.tk2[:], 15, None, AND))
+    v(V.tensor_scalar(T.kb[:], T.tk2[:], 4, None, AluOpType.arith_shift_right))
+    n = v(V.tensor_scalar(T.km[:], T.tk2[:], 0, None, AluOpType.is_lt))
+    V.wait_ge(m.v, n)
+    v(V.tensor_scalar(T.ka2[:], T.ka[:], 64, None, MUL))
+    n = v(V.tensor_tensor(T.kmu[:], T.km[:], T.ut[:], MUL))
+    V.wait_ge(m.v, n)
+    n = v(V.tensor_tensor(T.kc[:], T.ka2[:], T.kb[:], ADD))
+    V.wait_ge(m.v, n)
+    n = v(V.tensor_tensor(T.kd[:], T.kc[:], T.kmu[:], ADD))
+    V.wait_ge(m.v, n)
+    n = v(V.tensor_copy(T.so[:], T.kd[:]))
+    V.wait_ge(m.v, n)
+    v_inv = v(V.tensor_copy(T.inv[:, 0:1392].indirect(T.so[:, 0:16]), T.vals[:]))
+    V.wait_ge(m.d_tok, 128)
+    v_xo = v(V.tensor_scalar(T.xo[:], T.tokb[:], 0, 4, MAX, MUL))
+
+    blocks = [h] + [(h - o) % C for o in steps]
+
+    def xcols(blk):
+        return 16 * ranks[blocks[blk]][0], 16 * ranks[blocks[blk]][-1] + 16
+
+    def xgather(eng, blk, t):
+        a, b = xcols(blk)
+        win = T.xsb[:, t:4096].indirect(T.xo[:, a:b])
+        dst = T.hx[:, 64 * a + t:64 * b:4]
+        if eng == "v":
+            return v(V.tensor_copy(dst, win))
+        return s(S.activation(dst, win, COPY))
+
+    v_xq = {}
+
+    def xquant(blk):
+        a, b = xcols(blk)
+        v_xq[blk] = v(V.quantize_mx(T.xq[:, 16 * a:16 * b], T.xp[:, 16 * a:16 * b], T.hx[:, 64 * a:64 * b]))
+
+    S.wait_ge(m.v, v_xo)
+    S.wait_ge(m.d_x, 16)
+    for t in range(4):
+        s_xa = xgather("s", 0, t)
+    for t in range(2):
+        xgather("s", 2, t)
+    V.wait_ge(m.v, v_xo)
+    V.wait_ge(m.d_x, 16)
+    for t in range(4):
+        n = xgather("v", 1, t)
+    V.wait_ge(m.v, n)
+    xquant(1)
+    V.wait_ge(m.s, s_xa)
+    xquant(0)
+
+    Y.wait_ge(m.lleft, 1)
+    for k in range(8):
+        Y.dma_start(T.wab[:, 512 * k:512 * k + 512], T.wa[128 * k:128 * k + 128, :]).then_inc(m.d_wa, 16)
+    Y.wait_ge(m.v, v_inv)
+    for k in range(8):
+        Y.dma_start(T.e2[:, k, :], T.inv[16 * k:16 * k + 1, 0:1024]).then_inc(m.d_e1, 16)
+    Y.wait_ge(m.m_list, len(far))
+    Y.dma_start(T.tv1[0:1, :], T.tabl[0:6, 2 * rank:2 * rank + 2, :]).then_inc(m.d_r1, 16)
+    Y.wait_ge(m.d_own, 16)
+    Y.wait_ge(m.m_nl, len(off))
+    Y.dma_start(T.tv2[0:1, :], T.tabl[6:8, 2 * rank:2 * rank + 2, :]).then_inc(m.d_r2, 16)
+    Y.wait_ge(m.d_e1, 128)
+    for k in range(8):
+        Y.dma_start(T.mg[16 * k:16 * k + 16, :], T.e2[:]).then_inc(m.d_e2, 16)
+
+    g.wait_ge(m.d_r1, 16)
+    g_m1 = gq(g.partition_broadcast(T.tb1[:], T.tv1[0:1, :], 128))
+
+    def offsets(mf, a, dst):
+        return v(V.tensor_scalar(T.offu[:, 32 * dst:32 * dst + 32], T.base[:], mf[:, a:a + 1], None, ADD))
+
+    def agather(eng, a, b):
+        win = T.wab[:, 0:4096].indirect(T.offu[:, a // 16:b // 16])
+        if eng == "v":
+            return v(V.tensor_copy(T.ga[:, a:b], win))
+        return s(S.activation(T.ga[:, a:b], win, COPY))
+
+    V.wait_ge(m.gq, g_m1)
+    n = v(V.tensor_scalar(T.mf1[:], T.tb1[:], 0, 512, MAX, MUL))
+    V.wait_ge(m.v, n)
+    v_off = {}
+
+    def round_offsets(t):
+        for k in range(4):
+            v_off[t] = offsets(T.mf1, 4 * t + k, 4 * t + k)
+
+    round_offsets(0)
+    S.wait_ge(m.d_wa, 128)
+    r0, r1 = 256 * rank, 256 * rank + 256
+    for t in range(3):
+        if t + 1 < 3:
+            round_offsets(t + 1)
+        S.wait_ge(m.v, v_off[t])
+        s_g = agather("s", 2048 * t, 2048 * t + SSH)
+        V.wait_ge(m.v, v_off[t])
+        if t == 0:
+            V.wait_ge(m.d_wa, 128)
+        v_g = agather("v", 2048 * t + SSH, 2048 * t + 2048)
+        V.wait_ge(m.v, v_g)
+        V.wait_ge(m.s, s_g)
+        v_q = v(V.quantize_mx(T.aq[:, 512 * t:512 * t + 512], T.apl[:, 512 * t:512 * t + 512],
+                              T.ga[:, 2048 * t:2048 * t + 2048]))
+        rid, pid, _ = topo.addr(T.cores[out[t][0]])
+        direct = DstId(rid=rid, pnc=pid)
+        c0, c1, c2 = 512 * t, 512 * t + 256, 512 * t + 512
+        l0, l1 = 256 * t, 256 * t + 256
+        arr = m["arr%d" % rank]
+        g.wait_ge(m.v, v_q)
+        g.remote_dma_fused([
+            RemoteDMATransfer(dst_ids=[rly], dma_engine_mask=bits(inner), remote_sem=m["rc%d" % t],
+                              src=T.aq[:, c1:c2].bitcast(U8), dst=T.rlc[:, l0:l1].bitcast(U8)),
+            RemoteDMATransfer(dst_ids=[direct], dma_engine_mask=bits(off), remote_sem=arr,
+                              src=T.aq[:, c0:c1].bitcast(U8), dst=T.lc[:, r0:r1].bitcast(U8))], local_sem=m.sent)
+        g.remote_dma_fused([
+            RemoteDMATransfer(dst_ids=[rly], dma_engine_mask=bits(inner), remote_sem=m["rs%d" % t],
+                              src=T.apl[:, c1:c2], dst=T.rlp[:, l0:l1]),
+            RemoteDMATransfer(dst_ids=[direct], dma_engine_mask=bits(off), remote_sem=arr,
+                              src=T.apl[:, c0:c1], dst=T.lp[:, r0:r1])], local_sem=m.sent)
+        cnt["sent"] += 2 * (len(inner) + len(off))
+        if t == 0:
+            g.wait_ge(m.d_r2, 16)
+            g_m2 = gq(g.partition_broadcast(T.tb2[:], T.tv2[0:1, :], 128))
+        if t == 1:
+            V.wait_ge(m.gq, g_m2)
+            n = v(V.tensor_scalar(T.mf2[:], T.tb2[:], 0, 512, MAX, MUL))
+            V.wait_ge(m.v, n)
+            for k in range(4):
+                v_off2 = offsets(T.mf2, k, 12 + k)
+    S.wait_ge(m.v, v_off2)
+    s_n = agather("s", 6144, 7168)
+    s_o = agather("s", 7168, 8192)
+    V.wait_ge(m.s, s_n)
+    v_n = v(V.quantize_mx(T.aq[:, 1536:1792], T.apl[:, 1536:1792], T.ga[:, 6144:7168]))
+    rid, pid, _ = topo.addr(T.cores[nbr])
+    g.wait_ge(m.v, v_n)
+    g.remote_dma(T.lc[:, r0:r1].bitcast(U8), T.aq[:, 1536:1792].bitcast(U8), m["arr%d" % rank], m.sent, pid, rid, bits(inner))
+    g.remote_dma(T.lp[:, r0:r1], T.apl[:, 1536:1792], m["arr%d" % rank], m.sent, pid, rid, bits(inner))
+    cnt["sent"] += 2 * len(inner)
+    V.wait_ge(m.s, s_o)
+    v_o = v(V.quantize_mx(T.lc[:, r0:r1], T.lp[:, r0:r1], T.ga[:, 7168:8192]))
+
+    for t in (2, 3):
+        s_xc = xgather("s", 2, t)
+    for t in (0, 1):
+        s_xd = xgather("s", 3, t)
+    for t in (2, 3):
+        n = xgather("v", 3, t)
+    V.wait_ge(m.s, s_xc)
+    xquant(2)
+    V.wait_ge(m.s, s_xd)
+    V.wait_ge(m.v, n)
+    xquant(3)
+    V.wait_ge(m.d_e2, 128)
+    n = v(V.tensor_tensor(T.s1[:], T.mg[:, 0:256], T.mg[:, 256:512], ADD))
+    V.wait_ge(m.v, n)
+    n = v(V.tensor_tensor(T.s2[:], T.s1[:, 0:128], T.s1[:, 128:256], ADD))
+    V.wait_ge(m.v, n)
+    n = v(V.tensor_tensor(T.s3[:], T.s2[:, 0:64], T.s2[:, 64:128], ADD))
+    V.wait_ge(m.v, n)
+    v_yo = v(V.tensor_copy(T.yo[:], T.s3[:]))
+
+    order = [(rank, 0)] + [(q, 1) for q in src[0]] + [(q, 2) for q in src[1]] + [(nbr, 0)] + [(q, 3) for q in src[2]]
+    k = 0
+    freed, last = {}, {}
+    for q, blk in order:
+        if q == rank:
+            P.wait_ge(m.v, v_o)
+        else:
+            P.wait_ge(m["arr%d" % q], 2 * len(inner if q == nbr else off))
+        P.wait_ge(m.v, v_xq[blk])
+        for sl in (2 * q, 2 * q + 1):
+            bank = k % 8
+            if bank in freed:
+                P.wait_ge(m[freed[bank][0]], freed[bank][1])
+            a, b = 128 * sl, 128 * sl + 128
+            prod = T.ps[:, 512 * bank:512 * bank + 128]
+            did(P.matmul_mx(prod, T.lc[:, a:b], T.lp[:, a:b], T.xq[:, a:b], T.xp[:, a:b], True, True), "p")
+            if k % 2 == 0:
+                V.wait_ge(m.p, k + 1)
+                freed[bank] = ("v", v(V.tensor_copy(T.rsb[:, a:b], prod)))
+            else:
+                S.wait_ge(m.p, k + 1)
+                freed[bank] = ("s", s(S.activation(T.rsb[:, a:b], prod, COPY)))
+            last[freed[bank][0]] = freed[bank][1]
+            k += 1
+
+    for eng in (V, S):
+        eng.wait_ge(m.v, max(v_yo, last["v"]))
+        eng.wait_ge(m.s, last["s"])
+    n = v(V.tensor_copy(T.ysb[:, 0:512], T.rsb[:, 0:2048].indirect(T.yo[:, 0:32])))
+    Y.wait_ge(m.v, n)
+    Y.dma_start(T.y[:, 0:512], T.ysb[:, 0:512]).then_inc(m.d_y, 16)
+    n = s(S.activation(T.ysb[:, 512:1024], T.rsb[:, 0:2048].indirect(T.yo[:, 32:64]), COPY))
+    S.wait_ge(m.s, n)
+    S.dma_start(T.y[:, 512:1024], T.ysb[:, 512:1024]).then_inc(m.d_y, 16)
+
+    g.wait_ge(m.sent, cnt["sent"])
+    g.wait_ge(m.d_y, 32)
+    for name in ("v", "s", "p", "gq"):
+        g.wait_ge(m[name], cnt[name])

@@ -1,19 +1,19 @@
-from concourse.bass import DstId, RemoteDMATransfer
+from concourse.bass import DstId, RemoteDMATransfer, IndirectOffsetOnAxis
 from concourse.mybir import dt, AluOpType, ActivationFunctionType
 
 U8 = dt.uint8
 ADD, MUL, MAX, AND = AluOpType.add, AluOpType.mult, AluOpType.max, AluOpType.bitwise_and
 COPY = ActivationFunctionType.Copy
-SSH = 1280
 
 F8 = "float8_e4m3fn_x4"
 I16 = ("sbuf", [128, 16], "int32")
+I2 = ("sbuf", [128, 2], "int32")
 SCRATCH = {
-    "tabd": ("dram", [128, 1], "int32"), "tabl": ("dram", [8, 128, 1], "int32"), "rtab": ("dram", [128, 1], "int32"),
+    "tabd": ("dram", [128, 1], "int32"), "tabl": ("dram", [7, 128, 1], "int32"), "rtab": ("dram", [128, 1], "int32"),
     "tv1": ("sbuf", [128, 12], "int32"), "tb1": ("sbuf", [128, 12], "int32"), "mf1": ("sbuf", [128, 12], "float32"),
-    "tv2": ("sbuf", [128, 4], "int32"), "tb2": ("sbuf", [128, 4], "int32"), "mf2": ("sbuf", [128, 4], "float32"),
+    "tv2": I2, "tb2": I2, "mf2": ("sbuf", [128, 2], "float32"), "tv3": I2, "tb3": I2, "mi3": I2, "ix3": I2,
     "ibp": ("sbuf", [128, 32], "int32"), "ibc": ("sbuf", [128, 32], "int32"), "ibr": ("sbuf", [128, 32], "int32"),
-    "base": ("sbuf", [128, 32], "float32"), "offu": ("sbuf", [128, 512], "uint16"),
+    "base": ("sbuf", [128, 32], "float32"), "offu": ("sbuf", [128, 448], "uint16"),
     "tokb": ("sbuf", [128, 128], "int32"), "xo": ("sbuf", [128, 128], "uint16"),
     "tk2": I16, "ka": I16, "kb": I16, "km": I16, "ka2": I16, "kmu": I16, "kc": I16, "kd": I16, "ut": I16,
     "so": ("sbuf", [128, 16], "uint16"), "vals": ("sbuf", [128, 256], "float32"), "inv": ("sbuf", [128, 1392], "float32"),
@@ -21,15 +21,16 @@ SCRATCH = {
     "s2": ("sbuf", [128, 128], "float32"), "s3": ("sbuf", [128, 64], "float32"), "yo": ("sbuf", [128, 64], "uint16"),
     "wab": ("sbuf", [128, 4096], "bfloat16"), "xsb": ("sbuf", [128, 4096], "bfloat16"), "hx": ("sbuf", [128, 8192], "bfloat16"),
     "xq": ("sbuf", [128, 2048], F8), "xp": ("sbuf", [128, 2048], "uint8"),
-    "ga": ("sbuf", [128, 8192], "bfloat16"), "aq": ("sbuf", [128, 1792], F8), "apl": ("sbuf", [128, 1792], "uint8"),
+    "ga": ("sbuf", [128, 7168], "bfloat16"), "go": ("sbuf", [128, 1024], "bfloat16"),
+    "aq": ("sbuf", [128, 1792], F8), "apl": ("sbuf", [128, 1792], "uint8"),
     "lc": ("sbuf", [128, 2048], F8), "lp": ("sbuf", [128, 2048], "uint8"),
     "rlc": ("sbuf", [128, 768], F8), "rlp": ("sbuf", [128, 768], "uint8"),
     "rsb": ("sbuf", [128, 2048], "float32"), "ysb": ("sbuf", [128, 1024], "float32"),
     "ps": ("psum", [128, 4096], "float32"),
 }
-SEMAPHORES = (["d_tab", "d_own", "d_x", "d_tok", "d_tk2", "d_wa", "d_e1", "d_e2", "d_r1", "d_r2", "d_y",
-               "v", "s", "p", "gq", "lleft", "sent", "m_list", "m_nl", "rl"]
-              + ["arr%d" % q for q in range(8)] + ["rc%d" % t for t in range(3)] + ["rs%d" % t for t in range(3)])
+SEMAPHORES = (["d_tab", "d_own", "d_x", "d_tok", "d_tk2", "d_wa", "d_e1", "d_e2", "d_r1", "d_r2", "d_y", "d_go",
+               "v", "s", "p", "gq", "sent", "m_list", "m_nl", "rl"]
+              + ["rc%d" % k for k in range(3)] + ["rs%d" % k for k in range(3)] + ["arr%d" % q for q in range(8)])
 
 
 def bits(engines):
@@ -54,7 +55,11 @@ def relay_of(T, topo, core, place):
 
 def served(ranks, steps, h, i):
     n = len(ranks)
-    return [(ranks[(h + o) % n][i], ranks[(h + o) % n][1 - i]) for o in steps]
+    return [ranks[(h + o) % n][1 - i] for o in steps], [ranks[(h + o) % n][i] for o in steps]
+
+
+def in_order(rl, dr):
+    return [rl[0], rl[1], dr[0], rl[2], dr[1], dr[2]]
 
 
 def relay_program(g, core, T, topo):
@@ -67,23 +72,23 @@ def relay_program(g, core, T, topo):
             continue
         me = T.sem
         nb = T.cores[ranks[h][1 - i]]
-        dests = [T.cores[far] for near, far in served(ranks, steps, h, i)]
+        dests = [T.cores[q] for q in served(ranks, steps, h, i)[0]]
         eng = topo.engines(core, dests[0])
         on = topo.engines(T.cores[r], core)
-        ins = len([e for e in on if e not in topo.engines(T.cores[r], dests[0])])
+        inner = [e for e in on if e not in topo.engines(T.cores[r], dests[0])]
+        a, b = 256 * r, 256 * r + 256
+        arr = me["arr%d" % r]
         g.wait_ge(me.rl, len(on))
         rid, pid, _ = topo.addr(nb)
         g.remote_dma(T.tabl[6], T.rtab[:], me.m_nl, me.sent, pid, rid, bits(eng))
-        n = len(eng)
-        for t, d in enumerate(dests):
+        for k, d in enumerate(dests):
             rid, pid, _ = topo.addr(d)
-            a, b, c0, c1 = 256 * r, 256 * r + 256, 256 * t, 256 * t + 256
-            g.wait_ge(me["rc%d" % t], ins)
-            g.remote_dma(T.lc[:, a:b].bitcast(U8), T.rlc[:, c0:c1].bitcast(U8), me["arr%d" % r], me.sent, pid, rid, bits(eng))
-            g.wait_ge(me["rs%d" % t], ins)
-            g.remote_dma(T.lp[:, a:b], T.rlp[:, c0:c1], me["arr%d" % r], me.sent, pid, rid, bits(eng))
-            n += 2 * len(eng)
-        g.wait_ge(me.sent, n)
+            ins = len(inner if k else on)
+            g.wait_ge(me["rc%d" % k], ins)
+            g.remote_dma(T.lc[:, a:b].bitcast(U8), T.rlc[:, 256 * k:256 * k + 256].bitcast(U8), arr, me.sent, pid, rid, bits(eng))
+            g.wait_ge(me["rs%d" % k], ins)
+            g.remote_dma(T.lp[:, a:b], T.rlp[:, 256 * k:256 * k + 256], arr, me.sent, pid, rid, bits(eng))
+        g.wait_ge(me.sent, 7 * len(eng))
 
 
 def rank_program(g, core, T, topo):
@@ -96,10 +101,12 @@ def rank_program(g, core, T, topo):
     i = ranks[h].index(rank)
     nbr = ranks[h][1 - i]
     relay = relay_of(T, topo, core, i)
-    out = served(ranks, steps, h, i)
-    src = [(ranks[(h - o) % C][i], ranks[(h - o) % C][1 - i]) for o in steps]
+    relayed, direct = served(ranks, steps, h, i)
+    out = in_order(relayed, direct)
+    rsrc = [ranks[(h - o) % C][1 - i] for o in steps]
+    dsrc = [ranks[(h - o) % C][i] for o in steps]
     on = topo.engines(core, relay)
-    off = topo.engines(core, T.cores[out[0][0]])
+    off = topo.engines(core, T.cores[out[0]])
     inner = [e for e in on if e not in off]
     S, V, P, Y = g.scalar, g.vector, g.tensor, g.sync
     m = T.sem
@@ -114,42 +121,49 @@ def rank_program(g, core, T, topo):
     def s(ins): return did(ins, "s")
     def gq(ins): return did(ins, "gq")
 
+    def dst_id(c):
+        rid, pid, _ = topo.addr(c)
+        return DstId(rid=rid, pnc=pid)
+
     def place(q):
         hq = [k for k in range(C) if q in ranks[k]][0]
-        o = served(ranks, steps, hq, ranks[hq].index(q))
-        return [2 * t + k for t in range(len(o)) for k in range(2) if o[t][k] == rank][0]
+        return in_order(*served(ranks, steps, hq, ranks[hq].index(q))).index(rank)
+
+    def tok_loads(eng, ks):
+        for k in ks:
+            eng.dma_start(T.tk2[16 * k:16 * k + 16, :], T.tok[:, 16 * k:16 * k + 16]).then_inc(m.d_tk2, 16)
+        for k in ks:
+            eng.dma_start(T.tokb[16 * k:16 * k + 16, :], T.tok[:]).then_inc(m.d_tok, 16)
 
     Y.dma_start(T.tabd[0:16, :], T.tab[:]).then_inc(m.d_tab, 16)
     Y.dma_start(T.tabd[16:128, :], T.tok[0:1, 0:112]).then_inc(m.d_tab, 16)
+    S.dma_start(T.tv3[0:1, :], T.tab[2 * rank:2 * rank + 2, :]).then_inc(m.d_own, 16)
+    tok_loads(Y, range(0, 4))
+    tok_loads(S, range(4, 8))
     Y.dma_start(T.xsb[:], T.x[:]).then_inc(m.d_x, 16)
-    Y.dma_start(T.tabl[7, 0:16, :], T.tab[:]).then_inc(m.d_own, 16)
-    for k in range(8):
-        S.dma_start(T.tk2[16 * k:16 * k + 16, :], T.tok[:, 16 * k:16 * k + 16]).then_inc(m.d_tk2, 16)
-    for k in range(8):
-        S.dma_start(T.tokb[16 * k:16 * k + 16, :], T.tok[:]).then_inc(m.d_tok, 16)
     gq(g.iota(T.ut[:], [[16, 16]], 65, 1))
-    gq(g.iota(T.vals[:], [[1, 256]], 0, 16, allow_small_or_imprecise_dtypes=True))
     gq(g.iota(T.ibp[:], [[0, 32]], 0, 1))
-    g_b = gq(g.iota(T.ibc[:], [[16, 32]], 0, 0))
+    gq(g.iota(T.ibc[:], [[16, 32]], 0, 0))
+    g_b = gq(g.iota(T.vals[:], [[1, 256]], 0, 16, allow_small_or_imprecise_dtypes=True))
+    g.wait_ge(m.d_own, 16)
+    g_m3 = gq(g.partition_broadcast(T.tb3[:], T.tv3[0:1, :], 128))
     g.wait_ge(m.d_tab, 32)
-    far = [q for pair in out for q in pair]
-    ids, dsts = [], []
-    for q in far:
-        rid, pid, _ = topo.addr(T.cores[q])
-        ids.append(DstId(rid=rid, pnc=pid))
-        dsts.append(T.tabl[place(q)])
-    g.remote_dma_fused([RemoteDMATransfer(dst_ids=ids, dma_engine_mask=bits(off[:1]), remote_sem=m.m_list,
-                                          srcs=[T.tabd[:]], dsts=dsts)], local_sem=m.lleft)
+    g.remote_dma_fused([RemoteDMATransfer(dst_ids=[dst_id(T.cores[q]) for q in out], dma_engine_mask=bits(off[:1]),
+                                          remote_sem=m.m_list, srcs=[T.tabd[:]], dsts=[T.tabl[place(q)] for q in out])],
+                       local_sem=m.sent)
     rid, pid, _ = topo.addr(relay)
-    rly = DstId(rid=rid, pnc=pid)
     g.remote_dma(T.rtab[:], T.tabd[:], m.rl, m.sent, pid, rid, bits(on))
-    cnt["sent"] += len(on)
+    cnt["sent"] += 1 + len(on)
 
     v(V.memset(T.inv[:], 0.0))
     V.wait_ge(m.gq, g_b)
     n = v(V.tensor_scalar(T.ibr[:], T.ibp[:], 15, None, AND))
     V.wait_ge(m.v, n)
     v(V.tensor_tensor(T.base[:], T.ibr[:], T.ibc[:], ADD))
+    V.wait_ge(m.gq, g_m3)
+    n = v(V.tensor_scalar(T.mi3[:], T.tb3[:], 0, 128, MAX, MUL))
+    V.wait_ge(m.v, n)
+    v_ix = v(V.tensor_tensor(T.ix3[:], T.mi3[:], T.ibp[:, 0:2], ADD))
     V.wait_ge(m.d_tk2, 128)
     v(V.tensor_scalar(T.ka[:], T.tk2[:], 15, None, AND))
     v(V.tensor_scalar(T.kb[:], T.tk2[:], 4, None, AluOpType.arith_shift_right))
@@ -163,62 +177,63 @@ def rank_program(g, core, T, topo):
     n = v(V.tensor_tensor(T.kd[:], T.kc[:], T.kmu[:], ADD))
     V.wait_ge(m.v, n)
     n = v(V.tensor_copy(T.so[:], T.kd[:]))
-    V.wait_ge(m.v, n)
-    v_inv = v(V.tensor_copy(T.inv[:, 0:1392].indirect(T.so[:, 0:16]), T.vals[:]))
     V.wait_ge(m.d_tok, 128)
     v_xo = v(V.tensor_scalar(T.xo[:], T.tokb[:], 0, 4, MAX, MUL))
+    V.wait_ge(m.v, n)
+    v_inv = v(V.tensor_copy(T.inv[:, 0:1392].indirect(T.so[:, 0:16]), T.vals[:]))
 
-    blocks = [h] + [(h - o) % C for o in steps]
+    def own_rows(k):
+        g.indirect_dma_start(T.go[:, 512 * k:512 * k + 512], None, T.wa[:], IndirectOffsetOnAxis(ap=T.ix3[:, k:k + 1], axis=0),
+                             bounds_check=1023).then_inc(m.d_go, 16)
 
-    def xcols(blk):
-        return 16 * ranks[blocks[blk]][0], 16 * ranks[blocks[blk]][-1] + 16
+    g.wait_ge(m.v, v_ix)
+    own_rows(0)
 
-    def xgather(eng, blk, t):
-        a, b = xcols(blk)
-        win = T.xsb[:, t:4096].indirect(T.xo[:, a:b])
-        dst = T.hx[:, 64 * a + t:64 * b:4]
+    pairs = [h // 2, 1 - h // 2]
+
+    def xgather(eng, pr, t):
+        a = 64 * pairs[pr]
+        win = T.xsb[:, t:4096].indirect(T.xo[:, a:a + 64])
+        dst = T.hx[:, 64 * a + t:64 * a + 4096:4]
         if eng == "v":
             return v(V.tensor_copy(dst, win))
         return s(S.activation(dst, win, COPY))
 
+    def xquant(pr):
+        for a in (1024 * pairs[pr], 1024 * pairs[pr] + 512):
+            v_xq[pairs[pr]] = v(V.quantize_mx(T.xq[:, a:a + 512], T.xp[:, a:a + 512], T.hx[:, 4 * a:4 * a + 2048]))
+
     v_xq = {}
-
-    def xquant(blk):
-        a, b = xcols(blk)
-        v_xq[blk] = v(V.quantize_mx(T.xq[:, 16 * a:16 * b], T.xp[:, 16 * a:16 * b], T.hx[:, 64 * a:64 * b]))
-
     S.wait_ge(m.v, v_xo)
     S.wait_ge(m.d_x, 16)
-    for t in range(4):
-        s_xa = xgather("s", 0, t)
-    for t in range(2):
-        xgather("s", 2, t)
+    xgather("s", 0, 0)
+    s_x0 = xgather("s", 0, 1)
+    xgather("s", 1, 0)
     V.wait_ge(m.v, v_xo)
     V.wait_ge(m.d_x, 16)
-    for t in range(4):
-        n = xgather("v", 1, t)
+    xgather("v", 0, 2)
+    n = xgather("v", 0, 3)
     V.wait_ge(m.v, n)
-    xquant(1)
-    V.wait_ge(m.s, s_xa)
+    V.wait_ge(m.s, s_x0)
     xquant(0)
 
-    Y.wait_ge(m.lleft, 1)
+    Y.wait_ge(m.d_x, 16)
     for k in range(8):
         Y.dma_start(T.wab[:, 512 * k:512 * k + 512], T.wa[128 * k:128 * k + 128, :]).then_inc(m.d_wa, 16)
+    Y.wait_ge(m.m_list, len(out))
+    Y.dma_start(T.tv1[0:1, :], T.tabl[0:6, 2 * rank:2 * rank + 2, :]).then_inc(m.d_r1, 16)
+    Y.wait_ge(m.m_nl, len(off))
+    Y.dma_start(T.tv2[0:1, :], T.tabl[6, 2 * rank:2 * rank + 2, :]).then_inc(m.d_r2, 16)
     Y.wait_ge(m.v, v_inv)
     for k in range(8):
         Y.dma_start(T.e2[:, k, :], T.inv[16 * k:16 * k + 1, 0:1024]).then_inc(m.d_e1, 16)
-    Y.wait_ge(m.m_list, len(far))
-    Y.dma_start(T.tv1[0:1, :], T.tabl[0:6, 2 * rank:2 * rank + 2, :]).then_inc(m.d_r1, 16)
-    Y.wait_ge(m.d_own, 16)
-    Y.wait_ge(m.m_nl, len(off))
-    Y.dma_start(T.tv2[0:1, :], T.tabl[6:8, 2 * rank:2 * rank + 2, :]).then_inc(m.d_r2, 16)
     Y.wait_ge(m.d_e1, 128)
     for k in range(8):
         Y.dma_start(T.mg[16 * k:16 * k + 16, :], T.e2[:]).then_inc(m.d_e2, 16)
 
     g.wait_ge(m.d_r1, 16)
     g_m1 = gq(g.partition_broadcast(T.tb1[:], T.tv1[0:1, :], 128))
+    own_rows(1)
 
     def offsets(mf, a, dst):
         return v(V.tensor_scalar(T.offu[:, 32 * dst:32 * dst + 32], T.base[:], mf[:, a:a + 1], None, ADD))
@@ -233,95 +248,91 @@ def rank_program(g, core, T, topo):
     n = v(V.tensor_scalar(T.mf1[:], T.tb1[:], 0, 512, MAX, MUL))
     V.wait_ge(m.v, n)
     v_off = {}
+    rounds = [(0, 256), (256, 768), (768, 1280), (1280, 1792)]
 
     def round_offsets(t):
-        for k in range(4):
-            v_off[t] = offsets(T.mf1, 4 * t + k, 4 * t + k)
+        if t == 3:
+            V.wait_ge(m.gq, g_m2[0])
+            w = v(V.tensor_scalar(T.mf2[:], T.tb2[:], 0, 512, MAX, MUL))
+            offsets(T.mf1, 10, 12)
+            offsets(T.mf1, 11, 13)
+            V.wait_ge(m.v, w)
+            offsets(T.mf2, 0, 10)
+            v_off[t] = offsets(T.mf2, 1, 11)
+            return
+        for k in range(rounds[t][0] // 128, rounds[t][1] // 128):
+            v_off[t] = offsets(T.mf1, k, k)
 
+    g_m2 = []
     round_offsets(0)
     S.wait_ge(m.d_wa, 128)
     r0, r1 = 256 * rank, 256 * rank + 256
-    for t in range(3):
-        if t + 1 < 3:
+    arr = m["arr%d" % rank]
+    rly = dst_id(relay)
+    for t, (c0, c2) in enumerate(rounds):
+        if t + 1 < 4:
             round_offsets(t + 1)
+        e0, e2 = 4 * c0, 4 * c2
+        e1 = e0 + (e2 - e0) // 8 * 5
         S.wait_ge(m.v, v_off[t])
-        s_g = agather("s", 2048 * t, 2048 * t + SSH)
+        s_g = agather("s", e0, e1)
         V.wait_ge(m.v, v_off[t])
         if t == 0:
             V.wait_ge(m.d_wa, 128)
-        v_g = agather("v", 2048 * t + SSH, 2048 * t + 2048)
+        v_g = agather("v", e1, e2)
         V.wait_ge(m.v, v_g)
         V.wait_ge(m.s, s_g)
-        v_q = v(V.quantize_mx(T.aq[:, 512 * t:512 * t + 512], T.apl[:, 512 * t:512 * t + 512],
-                              T.ga[:, 2048 * t:2048 * t + 2048]))
-        rid, pid, _ = topo.addr(T.cores[out[t][0]])
-        direct = DstId(rid=rid, pnc=pid)
-        c0, c1, c2 = 512 * t, 512 * t + 256, 512 * t + 512
-        l0, l1 = 256 * t, 256 * t + 256
-        arr = m["arr%d" % rank]
+        v_q = v(V.quantize_mx(T.aq[:, c0:c2], T.apl[:, c0:c2], T.ga[:, e0:e2]))
         g.wait_ge(m.v, v_q)
-        g.remote_dma_fused([
-            RemoteDMATransfer(dst_ids=[rly], dma_engine_mask=bits(inner), remote_sem=m["rc%d" % t],
-                              src=T.aq[:, c1:c2].bitcast(U8), dst=T.rlc[:, l0:l1].bitcast(U8)),
-            RemoteDMATransfer(dst_ids=[direct], dma_engine_mask=bits(off), remote_sem=arr,
-                              src=T.aq[:, c0:c1].bitcast(U8), dst=T.lc[:, r0:r1].bitcast(U8))], local_sem=m.sent)
-        g.remote_dma_fused([
-            RemoteDMATransfer(dst_ids=[rly], dma_engine_mask=bits(inner), remote_sem=m["rs%d" % t],
-                              src=T.apl[:, c1:c2], dst=T.rlp[:, l0:l1]),
-            RemoteDMATransfer(dst_ids=[direct], dma_engine_mask=bits(off), remote_sem=arr,
-                              src=T.apl[:, c0:c1], dst=T.lp[:, r0:r1])], local_sem=m.sent)
-        cnt["sent"] += 2 * (len(inner) + len(off))
         if t == 0:
+            rid, pid, _ = topo.addr(relay)
+            g.remote_dma(T.rlc[:, 0:256].bitcast(U8), T.aq[:, c0:c2].bitcast(U8), m.rc0, m.sent, pid, rid, bits(on))
+            g.remote_dma(T.rlp[:, 0:256], T.apl[:, c0:c2], m.rs0, m.sent, pid, rid, bits(on))
+            cnt["sent"] += 2 * len(on)
             g.wait_ge(m.d_r2, 16)
-            g_m2 = gq(g.partition_broadcast(T.tb2[:], T.tv2[0:1, :], 128))
-        if t == 1:
-            V.wait_ge(m.gq, g_m2)
-            n = v(V.tensor_scalar(T.mf2[:], T.tb2[:], 0, 512, MAX, MUL))
-            V.wait_ge(m.v, n)
-            for k in range(4):
-                v_off2 = offsets(T.mf2, k, 12 + k)
-    S.wait_ge(m.v, v_off2)
-    s_n = agather("s", 6144, 7168)
-    s_o = agather("s", 7168, 8192)
-    V.wait_ge(m.s, s_n)
-    v_n = v(V.quantize_mx(T.aq[:, 1536:1792], T.apl[:, 1536:1792], T.ga[:, 6144:7168]))
-    rid, pid, _ = topo.addr(T.cores[nbr])
-    g.wait_ge(m.v, v_n)
-    g.remote_dma(T.lc[:, r0:r1].bitcast(U8), T.aq[:, 1536:1792].bitcast(U8), m["arr%d" % rank], m.sent, pid, rid, bits(inner))
-    g.remote_dma(T.lp[:, r0:r1], T.apl[:, 1536:1792], m["arr%d" % rank], m.sent, pid, rid, bits(inner))
-    cnt["sent"] += 2 * len(inner)
-    V.wait_ge(m.s, s_o)
-    v_o = v(V.quantize_mx(T.lc[:, r0:r1], T.lp[:, r0:r1], T.ga[:, 7168:8192]))
+            g_m2.append(gq(g.partition_broadcast(T.tb2[:], T.tv2[0:1, :], 128)))
+            continue
+        c1 = c0 + 256
+        to = [(dst_id(T.cores[direct[t - 1]]), off, arr, T.lc[:, r0:r1], arr, T.lp[:, r0:r1], c1, c2)]
+        if t < 3:
+            to.insert(0, (rly, inner, m["rc%d" % t], T.rlc[:, 256 * t:256 * t + 256],
+                          m["rs%d" % t], T.rlp[:, 256 * t:256 * t + 256], c0, c1))
+        else:
+            to.append((dst_id(T.cores[nbr]), inner, arr, T.lc[:, r0:r1], arr, T.lp[:, r0:r1], c0, c1))
+        g.remote_dma_fused([RemoteDMATransfer(dst_ids=[d], dma_engine_mask=bits(e), remote_sem=sc,
+                                              src=T.aq[:, a:b].bitcast(U8), dst=lc.bitcast(U8))
+                            for d, e, sc, lc, ss, lp, a, b in to], local_sem=m.sent)
+        g.remote_dma_fused([RemoteDMATransfer(dst_ids=[d], dma_engine_mask=bits(e), remote_sem=ss, src=T.apl[:, a:b], dst=lp)
+                            for d, e, sc, lc, ss, lp, a, b in to], local_sem=m.sent)
+        cnt["sent"] += 2 * (len(off) + len(inner))
+    V.wait_ge(m.d_go, 32)
+    v_o = v(V.quantize_mx(T.lc[:, r0:r1], T.lp[:, r0:r1], T.go[:]))
 
-    for t in (2, 3):
-        s_xc = xgather("s", 2, t)
-    for t in (0, 1):
-        s_xd = xgather("s", 3, t)
-    for t in (2, 3):
-        n = xgather("v", 3, t)
-    V.wait_ge(m.s, s_xc)
-    xquant(2)
-    V.wait_ge(m.s, s_xd)
-    V.wait_ge(m.v, n)
-    xquant(3)
+    xgather("s", 1, 1)
+    s_x1 = xgather("s", 1, 2)
+    n = xgather("v", 1, 3)
     V.wait_ge(m.d_e2, 128)
-    n = v(V.tensor_tensor(T.s1[:], T.mg[:, 0:256], T.mg[:, 256:512], ADD))
-    V.wait_ge(m.v, n)
-    n = v(V.tensor_tensor(T.s2[:], T.s1[:, 0:128], T.s1[:, 128:256], ADD))
-    V.wait_ge(m.v, n)
-    n = v(V.tensor_tensor(T.s3[:], T.s2[:, 0:64], T.s2[:, 64:128], ADD))
-    V.wait_ge(m.v, n)
+    k = v(V.tensor_tensor(T.s1[:], T.mg[:, 0:256], T.mg[:, 256:512], ADD))
+    V.wait_ge(m.v, k)
+    k = v(V.tensor_tensor(T.s2[:], T.s1[:, 0:128], T.s1[:, 128:256], ADD))
+    V.wait_ge(m.v, k)
+    k = v(V.tensor_tensor(T.s3[:], T.s2[:, 0:64], T.s2[:, 64:128], ADD))
+    V.wait_ge(m.v, k)
     v_yo = v(V.tensor_copy(T.yo[:], T.s3[:]))
+    V.wait_ge(m.s, s_x1)
+    V.wait_ge(m.v, n)
+    xquant(1)
 
-    order = [(rank, 0)] + [(q, 1) for q in src[0]] + [(q, 2) for q in src[1]] + [(nbr, 0)] + [(q, 3) for q in src[2]]
+    f = [k for k in (0, 1) if dsrc[k] // 4 == rank // 4][0]
+    order = [rank, dsrc[f], rsrc[f], nbr, dsrc[1 - f], rsrc[1 - f], dsrc[2], rsrc[2]]
     k = 0
     freed, last = {}, {}
-    for q, blk in order:
+    for q in order:
         if q == rank:
             P.wait_ge(m.v, v_o)
         else:
             P.wait_ge(m["arr%d" % q], 2 * len(inner if q == nbr else off))
-        P.wait_ge(m.v, v_xq[blk])
+        P.wait_ge(m.v, v_xq[q // 4])
         for sl in (2 * q, 2 * q + 1):
             bank = k % 8
             if bank in freed:
@@ -341,14 +352,24 @@ def rank_program(g, core, T, topo):
     for eng in (V, S):
         eng.wait_ge(m.v, max(v_yo, last["v"]))
         eng.wait_ge(m.s, last["s"])
-    n = v(V.tensor_copy(T.ysb[:, 0:512], T.rsb[:, 0:2048].indirect(T.yo[:, 0:32])))
-    Y.wait_ge(m.v, n)
-    Y.dma_start(T.y[:, 0:512], T.ysb[:, 0:512]).then_inc(m.d_y, 16)
-    n = s(S.activation(T.ysb[:, 512:1024], T.rsb[:, 0:2048].indirect(T.yo[:, 32:64]), COPY))
-    S.wait_ge(m.s, n)
-    S.dma_start(T.y[:, 512:1024], T.ysb[:, 512:1024]).then_inc(m.d_y, 16)
+
+    def picked(k):
+        return T.ysb[:, 256 * k:256 * k + 256], T.rsb[:, 0:2048].indirect(T.yo[:, 16 * k:16 * k + 16])
+
+    vn, sn = [], []
+    for k in range(2):
+        vn.append(v(V.tensor_copy(*picked(k))))
+        o, w = picked(2 + k)
+        sn.append(s(S.activation(o, w, COPY)))
+    for k in range(2):
+        Y.wait_ge(m.v, vn[k])
+        Y.dma_start(T.y[:, 256 * k:256 * k + 256], T.ysb[:, 256 * k:256 * k + 256]).then_inc(m.d_y, 16)
+    for k in range(2):
+        S.wait_ge(m.s, sn[k])
+        S.dma_start(T.y[:, 512 + 256 * k:768 + 256 * k], T.ysb[:, 512 + 256 * k:768 + 256 * k]).then_inc(m.d_y, 16)
 
     g.wait_ge(m.sent, cnt["sent"])
-    g.wait_ge(m.d_y, 32)
+    g.wait_ge(m.d_y, 64)
+    g.wait_ge(m.d_go, 32)
     for name in ("v", "s", "p", "gq"):
         g.wait_ge(m[name], cnt[name])

from concourse.bass import DstId, RemoteDMATransfer, IndirectOffsetOnAxis
from concourse.mybir import dt, AluOpType, ActivationFunctionType

U8 = dt.uint8
ADD, MUL, MAX, AND = AluOpType.add, AluOpType.mult, AluOpType.max, AluOpType.bitwise_and
COPY = ActivationFunctionType.Copy

F8 = "float8_e4m3fn_x4"
I16 = ("sbuf", [128, 16], "int32")
I2 = ("sbuf", [128, 2], "int32")
SCRATCH = {
    "tabd": ("dram", [128, 1], "int32"), "tabl": ("dram", [7, 128, 1], "int32"), "rtab": ("dram", [128, 1], "int32"),
    "tv1": ("sbuf", [128, 12], "int32"), "tb1": ("sbuf", [128, 12], "int32"), "mf1": ("sbuf", [128, 12], "float32"),
    "tv2": I2, "tb2": I2, "mf2": ("sbuf", [128, 2], "float32"), "tv3": I2, "tb3": I2, "mi3": I2, "ix3": I2,
    "ibp": ("sbuf", [128, 32], "int32"), "ibc": ("sbuf", [128, 32], "int32"), "ibr": ("sbuf", [128, 32], "int32"),
    "base": ("sbuf", [128, 32], "float32"), "offu": ("sbuf", [128, 448], "uint16"),
    "tokb": ("sbuf", [128, 128], "int32"), "xo": ("sbuf", [128, 128], "uint16"),
    "tk2": I16, "ka": I16, "kb": I16, "km": I16, "ka2": I16, "kmu": I16, "kc": I16, "kd": I16, "ut": I16,
    "so": ("sbuf", [128, 16], "uint16"), "vals": ("sbuf", [128, 256], "float32"), "inv": ("sbuf", [128, 1392], "float32"),
    "e2": ("dram", [16, 8, 64], "float32"), "mg": ("sbuf", [128, 512], "float32"), "s1": ("sbuf", [128, 256], "float32"),
    "s2": ("sbuf", [128, 128], "float32"), "s3": ("sbuf", [128, 64], "float32"), "yo": ("sbuf", [128, 64], "uint16"),
    "wab": ("sbuf", [128, 4096], "bfloat16"), "xsb": ("sbuf", [128, 4096], "bfloat16"), "hx": ("sbuf", [128, 8192], "bfloat16"),
    "xq": ("sbuf", [128, 2048], F8), "xp": ("sbuf", [128, 2048], "uint8"),
    "ga": ("sbuf", [128, 7168], "bfloat16"), "go": ("sbuf", [128, 1024], "bfloat16"),
    "aq": ("sbuf", [128, 1792], F8), "apl": ("sbuf", [128, 1792], "uint8"),
    "lc": ("sbuf", [128, 2048], F8), "lp": ("sbuf", [128, 2048], "uint8"),
    "rlc": ("sbuf", [128, 768], F8), "rlp": ("sbuf", [128, 768], "uint8"),
    "rsb": ("sbuf", [128, 2048], "float32"), "ysb": ("sbuf", [128, 1024], "float32"),
    "ps": ("psum", [128, 4096], "float32"),
}
SEMAPHORES = (["d_tab", "d_own", "d_x", "d_tok", "d_tk2", "d_wa", "d_e1", "d_e2", "d_r1", "d_r2", "d_y", "d_go",
               "v", "s", "p", "gq", "sent", "m_list", "m_nl", "rl"]
              + ["rc%d" % k for k in range(3)] + ["rs%d" % k for k in range(3)] + ["arr%d" % q for q in range(8)])


def bits(engines):
    return sum(1 << e for e in engines)


def layout(T, topo):
    chips = []
    for c in T.cores:
        if topo.chip(c) not in chips:
            chips.append(topo.chip(c))
    ranks = [[r for r, c in enumerate(T.cores) if topo.chip(c) == ch] for ch in chips]
    steps = sorted(range(1, len(chips)), key=lambda o: topo.same_plane(chips[0], chips[o]))
    return chips, ranks, steps


def relay_of(T, topo, core, place):
    c = [k for k in topo.cores_of(core) if topo.die(k) != topo.die(core) and T.rank_of(k) is None
         and all(topo.may_write(k, d) for d in T.cores)]
    return c[place]


def served(ranks, steps, h, i):
    n = len(ranks)
    return [ranks[(h + o) % n][1 - i] for o in steps], [ranks[(h + o) % n][i] for o in steps]


def in_order(rl, dr):
    return [rl[0], rl[1], dr[0], rl[2], dr[1], dr[2]]


def relay_program(g, core, T, topo):
    chips, ranks, steps = layout(T, topo)
    if topo.chip(core) not in chips:
        return
    h = chips.index(topo.chip(core))
    for i, r in enumerate(ranks[h]):
        if relay_of(T, topo, T.cores[r], i) != core:
            continue
        me = T.sem
        nb = T.cores[ranks[h][1 - i]]
        dests = [T.cores[q] for q in served(ranks, steps, h, i)[0]]
        eng = topo.engines(core, dests[0])
        on = topo.engines(T.cores[r], core)
        inner = [e for e in on if e not in topo.engines(T.cores[r], dests[0])]
        a, b = 256 * r, 256 * r + 256
        arr = me["arr%d" % r]
        g.wait_ge(me.rl, len(on))
        rid, pid, _ = topo.addr(nb)
        g.remote_dma(T.tabl[6], T.rtab[:], me.m_nl, me.sent, pid, rid, bits(eng))
        for k, d in enumerate(dests):
            rid, pid, _ = topo.addr(d)
            ins = len(inner if k else on)
            g.wait_ge(me["rc%d" % k], ins)
            g.remote_dma(T.lc[:, a:b].bitcast(U8), T.rlc[:, 256 * k:256 * k + 256].bitcast(U8), arr, me.sent, pid, rid, bits(eng))
            g.wait_ge(me["rs%d" % k], ins)
            g.remote_dma(T.lp[:, a:b], T.rlp[:, 256 * k:256 * k + 256], arr, me.sent, pid, rid, bits(eng))
        g.wait_ge(me.sent, 7 * len(eng))


def rank_program(g, core, T, topo):
    rank = T.rank_of(core)
    if rank is None:
        return relay_program(g, core, T, topo)
    chips, ranks, steps = layout(T, topo)
    C = len(chips)
    h = chips.index(topo.chip(core))
    i = ranks[h].index(rank)
    nbr = ranks[h][1 - i]
    relay = relay_of(T, topo, core, i)
    relayed, direct = served(ranks, steps, h, i)
    out = in_order(relayed, direct)
    rsrc = [ranks[(h - o) % C][1 - i] for o in steps]
    dsrc = [ranks[(h - o) % C][i] for o in steps]
    on = topo.engines(core, relay)
    off = topo.engines(core, T.cores[out[0]])
    inner = [e for e in on if e not in off]
    S, V, P, Y = g.scalar, g.vector, g.tensor, g.sync
    m = T.sem
    cnt = {"v": 0, "s": 0, "p": 0, "gq": 0, "sent": 0}

    def did(ins, name):
        ins.then_inc(m[name], 1)
        cnt[name] += 1
        return cnt[name]

    def v(ins): return did(ins, "v")
    def s(ins): return did(ins, "s")
    def gq(ins): return did(ins, "gq")

    def dst_id(c):
        rid, pid, _ = topo.addr(c)
        return DstId(rid=rid, pnc=pid)

    def place(q):
        hq = [k for k in range(C) if q in ranks[k]][0]
        return in_order(*served(ranks, steps, hq, ranks[hq].index(q))).index(rank)

    def tok_loads(eng, ks):
        for k in ks:
            eng.dma_start(T.tk2[16 * k:16 * k + 16, :], T.tok[:, 16 * k:16 * k + 16]).then_inc(m.d_tk2, 16)
        for k in ks:
            eng.dma_start(T.tokb[16 * k:16 * k + 16, :], T.tok[:]).then_inc(m.d_tok, 16)

    Y.dma_start(T.tabd[0:16, :], T.tab[:]).then_inc(m.d_tab, 16)
    Y.dma_start(T.tabd[16:128, :], T.tok[0:1, 0:112]).then_inc(m.d_tab, 16)
    S.dma_start(T.tv3[0:1, :], T.tab[2 * rank:2 * rank + 2, :]).then_inc(m.d_own, 16)
    tok_loads(Y, range(0, 4))
    tok_loads(S, range(4, 8))
    Y.dma_start(T.xsb[:], T.x[:]).then_inc(m.d_x, 16)
    gq(g.iota(T.ut[:], [[16, 16]], 65, 1))
    gq(g.iota(T.ibp[:], [[0, 32]], 0, 1))
    gq(g.iota(T.ibc[:], [[16, 32]], 0, 0))
    g_b = gq(g.iota(T.vals[:], [[1, 256]], 0, 16, allow_small_or_imprecise_dtypes=True))
    g.wait_ge(m.d_own, 16)
    g_m3 = gq(g.partition_broadcast(T.tb3[:], T.tv3[0:1, :], 128))
    g.wait_ge(m.d_tab, 32)
    g.remote_dma_fused([RemoteDMATransfer(dst_ids=[dst_id(T.cores[q]) for q in out], dma_engine_mask=bits(off[:1]),
                                          remote_sem=m.m_list, srcs=[T.tabd[:]], dsts=[T.tabl[place(q)] for q in out])],
                       local_sem=m.sent)
    rid, pid, _ = topo.addr(relay)
    g.remote_dma(T.rtab[:], T.tabd[:], m.rl, m.sent, pid, rid, bits(on))
    cnt["sent"] += 1 + len(on)

    v(V.memset(T.inv[:], 0.0))
    V.wait_ge(m.gq, g_b)
    n = v(V.tensor_scalar(T.ibr[:], T.ibp[:], 15, None, AND))
    V.wait_ge(m.v, n)
    v(V.tensor_tensor(T.base[:], T.ibr[:], T.ibc[:], ADD))
    V.wait_ge(m.gq, g_m3)
    n = v(V.tensor_scalar(T.mi3[:], T.tb3[:], 0, 128, MAX, MUL))
    V.wait_ge(m.v, n)
    v_ix = v(V.tensor_tensor(T.ix3[:], T.mi3[:], T.ibp[:, 0:2], ADD))
    V.wait_ge(m.d_tk2, 128)
    v(V.tensor_scalar(T.ka[:], T.tk2[:], 15, None, AND))
    v(V.tensor_scalar(T.kb[:], T.tk2[:], 4, None, AluOpType.arith_shift_right))
    n = v(V.tensor_scalar(T.km[:], T.tk2[:], 0, None, AluOpType.is_lt))
    V.wait_ge(m.v, n)
    v(V.tensor_scalar(T.ka2[:], T.ka[:], 64, None, MUL))
    n = v(V.tensor_tensor(T.kmu[:], T.km[:], T.ut[:], MUL))
    V.wait_ge(m.v, n)
    n = v(V.tensor_tensor(T.kc[:], T.ka2[:], T.kb[:], ADD))
    V.wait_ge(m.v, n)
    n = v(V.tensor_tensor(T.kd[:], T.kc[:], T.kmu[:], ADD))
    V.wait_ge(m.v, n)
    n = v(V.tensor_copy(T.so[:], T.kd[:]))
    V.wait_ge(m.d_tok, 128)
    v_xo = v(V.tensor_scalar(T.xo[:], T.tokb[:], 0, 4, MAX, MUL))
    V.wait_ge(m.v, n)
    v_inv = v(V.tensor_copy(T.inv[:, 0:1392].indirect(T.so[:, 0:16]), T.vals[:]))

    def own_rows(k):
        g.indirect_dma_start(T.go[:, 512 * k:512 * k + 512], None, T.wa[:], IndirectOffsetOnAxis(ap=T.ix3[:, k:k + 1], axis=0),
                             bounds_check=1023).then_inc(m.d_go, 16)

    g.wait_ge(m.v, v_ix)
    own_rows(0)

    pairs = [h // 2, 1 - h // 2]

    def xgather(eng, pr, t):
        a = 64 * pairs[pr]
        win = T.xsb[:, t:4096].indirect(T.xo[:, a:a + 64])
        dst = T.hx[:, 64 * a + t:64 * a + 4096:4]
        if eng == "v":
            return v(V.tensor_copy(dst, win))
        return s(S.activation(dst, win, COPY))

    def xquant(pr):
        for a in (1024 * pairs[pr], 1024 * pairs[pr] + 512):
            v_xq[pairs[pr]] = v(V.quantize_mx(T.xq[:, a:a + 512], T.xp[:, a:a + 512], T.hx[:, 4 * a:4 * a + 2048]))

    v_xq = {}
    S.wait_ge(m.v, v_xo)
    S.wait_ge(m.d_x, 16)
    xgather("s", 0, 0)
    s_x0 = xgather("s", 0, 1)
    xgather("s", 1, 0)
    V.wait_ge(m.v, v_xo)
    V.wait_ge(m.d_x, 16)
    xgather("v", 0, 2)
    n = xgather("v", 0, 3)
    V.wait_ge(m.v, n)
    V.wait_ge(m.s, s_x0)
    xquant(0)

    Y.wait_ge(m.d_x, 16)
    for k in range(8):
        Y.dma_start(T.wab[:, 512 * k:512 * k + 512], T.wa[128 * k:128 * k + 128, :]).then_inc(m.d_wa, 16)
    Y.wait_ge(m.m_list, len(out))
    Y.dma_start(T.tv1[0:1, :], T.tabl[0:6, 2 * rank:2 * rank + 2, :]).then_inc(m.d_r1, 16)
    Y.wait_ge(m.m_nl, len(off))
    Y.dma_start(T.tv2[0:1, :], T.tabl[6, 2 * rank:2 * rank + 2, :]).then_inc(m.d_r2, 16)
    Y.wait_ge(m.v, v_inv)
    for k in range(8):
        Y.dma_start(T.e2[:, k, :], T.inv[16 * k:16 * k + 1, 0:1024]).then_inc(m.d_e1, 16)
    Y.wait_ge(m.d_e1, 128)
    for k in range(8):
        Y.dma_start(T.mg[16 * k:16 * k + 16, :], T.e2[:]).then_inc(m.d_e2, 16)

    g.wait_ge(m.d_r1, 16)
    g_m1 = gq(g.partition_broadcast(T.tb1[:], T.tv1[0:1, :], 128))
    own_rows(1)

    def offsets(mf, a, dst):
        return v(V.tensor_scalar(T.offu[:, 32 * dst:32 * dst + 32], T.base[:], mf[:, a:a + 1], None, ADD))

    def agather(eng, a, b):
        win = T.wab[:, 0:4096].indirect(T.offu[:, a // 16:b // 16])
        if eng == "v":
            return v(V.tensor_copy(T.ga[:, a:b], win))
        return s(S.activation(T.ga[:, a:b], win, COPY))

    V.wait_ge(m.gq, g_m1)
    n = v(V.tensor_scalar(T.mf1[:], T.tb1[:], 0, 512, MAX, MUL))
    V.wait_ge(m.v, n)
    v_off = {}
    rounds = [(0, 256), (256, 768), (768, 1280), (1280, 1792)]

    def round_offsets(t):
        if t == 3:
            V.wait_ge(m.gq, g_m2[0])
            w = v(V.tensor_scalar(T.mf2[:], T.tb2[:], 0, 512, MAX, MUL))
            offsets(T.mf1, 10, 12)
            offsets(T.mf1, 11, 13)
            V.wait_ge(m.v, w)
            offsets(T.mf2, 0, 10)
            v_off[t] = offsets(T.mf2, 1, 11)
            return
        for k in range(rounds[t][0] // 128, rounds[t][1] // 128):
            v_off[t] = offsets(T.mf1, k, k)

    g_m2 = []
    round_offsets(0)
    S.wait_ge(m.d_wa, 128)
    r0, r1 = 256 * rank, 256 * rank + 256
    arr = m["arr%d" % rank]
    rly = dst_id(relay)
    for t, (c0, c2) in enumerate(rounds):
        if t + 1 < 4:
            round_offsets(t + 1)
        e0, e2 = 4 * c0, 4 * c2
        e1 = e0 + (e2 - e0) // 8 * 5
        S.wait_ge(m.v, v_off[t])
        s_g = agather("s", e0, e1)
        V.wait_ge(m.v, v_off[t])
        if t == 0:
            V.wait_ge(m.d_wa, 128)
        v_g = agather("v", e1, e2)
        V.wait_ge(m.v, v_g)
        V.wait_ge(m.s, s_g)
        v_q = v(V.quantize_mx(T.aq[:, c0:c2], T.apl[:, c0:c2], T.ga[:, e0:e2]))
        g.wait_ge(m.v, v_q)
        if t == 0:
            rid, pid, _ = topo.addr(relay)
            g.remote_dma(T.rlc[:, 0:256].bitcast(U8), T.aq[:, c0:c2].bitcast(U8), m.rc0, m.sent, pid, rid, bits(on))
            g.remote_dma(T.rlp[:, 0:256], T.apl[:, c0:c2], m.rs0, m.sent, pid, rid, bits(on))
            cnt["sent"] += 2 * len(on)
            g.wait_ge(m.d_r2, 16)
            g_m2.append(gq(g.partition_broadcast(T.tb2[:], T.tv2[0:1, :], 128)))
            continue
        c1 = c0 + 256
        to = [(dst_id(T.cores[direct[t - 1]]), off, arr, T.lc[:, r0:r1], arr, T.lp[:, r0:r1], c1, c2)]
        if t < 3:
            to.insert(0, (rly, inner, m["rc%d" % t], T.rlc[:, 256 * t:256 * t + 256],
                          m["rs%d" % t], T.rlp[:, 256 * t:256 * t + 256], c0, c1))
        else:
            to.append((dst_id(T.cores[nbr]), inner, arr, T.lc[:, r0:r1], arr, T.lp[:, r0:r1], c0, c1))
        g.remote_dma_fused([RemoteDMATransfer(dst_ids=[d], dma_engine_mask=bits(e), remote_sem=sc,
                                              src=T.aq[:, a:b].bitcast(U8), dst=lc.bitcast(U8))
                            for d, e, sc, lc, ss, lp, a, b in to], local_sem=m.sent)
        g.remote_dma_fused([RemoteDMATransfer(dst_ids=[d], dma_engine_mask=bits(e), remote_sem=ss, src=T.apl[:, a:b], dst=lp)
                            for d, e, sc, lc, ss, lp, a, b in to], local_sem=m.sent)
        cnt["sent"] += 2 * (len(off) + len(inner))
    V.wait_ge(m.d_go, 32)
    v_o = v(V.quantize_mx(T.lc[:, r0:r1], T.lp[:, r0:r1], T.go[:]))

    xgather("s", 1, 1)
    s_x1 = xgather("s", 1, 2)
    n = xgather("v", 1, 3)
    V.wait_ge(m.d_e2, 128)
    k = v(V.tensor_tensor(T.s1[:], T.mg[:, 0:256], T.mg[:, 256:512], ADD))
    V.wait_ge(m.v, k)
    k = v(V.tensor_tensor(T.s2[:], T.s1[:, 0:128], T.s1[:, 128:256], ADD))
    V.wait_ge(m.v, k)
    k = v(V.tensor_tensor(T.s3[:], T.s2[:, 0:64], T.s2[:, 64:128], ADD))
    V.wait_ge(m.v, k)
    v_yo = v(V.tensor_copy(T.yo[:], T.s3[:]))
    V.wait_ge(m.s, s_x1)
    V.wait_ge(m.v, n)
    xquant(1)

    f = [k for k in (0, 1) if dsrc[k] // 4 == rank // 4][0]
    order = [rank, dsrc[f], rsrc[f], nbr, dsrc[1 - f], rsrc[1 - f], dsrc[2], rsrc[2]]
    k = 0
    freed, last = {}, {}
    for q in order:
        if q == rank:
            P.wait_ge(m.v, v_o)
        else:
            P.wait_ge(m["arr%d" % q], 2 * len(inner if q == nbr else off))
        P.wait_ge(m.v, v_xq[q // 4])
        for sl in (2 * q, 2 * q + 1):
            bank = k % 8
            if bank in freed:
                P.wait_ge(m[freed[bank][0]], freed[bank][1])
            a, b = 128 * sl, 128 * sl + 128
            prod = T.ps[:, 512 * bank:512 * bank + 128]
            did(P.matmul_mx(prod, T.lc[:, a:b], T.lp[:, a:b], T.xq[:, a:b], T.xp[:, a:b], True, True), "p")
            if k % 2 == 0:
                V.wait_ge(m.p, k + 1)
                freed[bank] = ("v", v(V.tensor_copy(T.rsb[:, a:b], prod)))
            else:
                S.wait_ge(m.p, k + 1)
                freed[bank] = ("s", s(S.activation(T.rsb[:, a:b], prod, COPY)))
            last[freed[bank][0]] = freed[bank][1]
            k += 1

    for eng in (V, S):
        eng.wait_ge(m.v, max(v_yo, last["v"]))
        eng.wait_ge(m.s, last["s"])

    def picked(k):
        return T.ysb[:, 256 * k:256 * k + 256], T.rsb[:, 0:2048].indirect(T.yo[:, 16 * k:16 * k + 16])

    vn, sn = [], []
    for k in range(2):
        vn.append(v(V.tensor_copy(*picked(k))))
        o, w = picked(2 + k)
        sn.append(s(S.activation(o, w, COPY)))
    for k in range(2):
        Y.wait_ge(m.v, vn[k])
        Y.dma_start(T.y[:, 256 * k:256 * k + 256], T.ysb[:, 256 * k:256 * k + 256]).then_inc(m.d_y, 16)
    for k in range(2):
        S.wait_ge(m.s, sn[k])
        S.dma_start(T.y[:, 512 + 256 * k:768 + 256 * k], T.ysb[:, 512 + 256 * k:768 + 256 * k]).then_inc(m.d_y, 16)

    g.wait_ge(m.sent, cnt["sent"])
    g.wait_ge(m.d_y, 64)
    g.wait_ge(m.d_go, 32)
    for name in ("v", "s", "p", "gq"):
        g.wait_ge(m[name], cnt[name])
